import numpy as np
import ml_dtypes


def mxq(x, axis, fmt="e4m3"):
    dtype, down = {"e4m3": (ml_dtypes.float8_e4m3fn, 7), "e5m2": (ml_dtypes.float8_e5m2, 14)}[fmt]
    v = np.moveaxis(np.asarray(x, np.float32).astype(ml_dtypes.bfloat16).astype(np.float64), axis, -1)
    blocks = v.reshape(v.shape[:-1] + (-1, 32))
    amax = np.abs(blocks).max(-1, keepdims=True)
    byte = np.maximum(np.where(amax > 0, np.frexp(amax)[1] - 1 + 127, 0) - down, 1)
    scale = np.exp2(byte - 127.0)
    codes = (blocks / scale).astype(np.float32).astype(dtype).astype(np.float64)
    return np.moveaxis((codes * scale).reshape(v.shape), -1, axis)


WIDE = False


def mx_kscale(k):
    if not WIDE:
        return np.ones(k)
    levels = np.array([10, -10, 5, -5, 0])
    if k % 512:
        return np.exp2(np.random.permutation(np.resize(levels, k // 32))).repeat(32)
    a = np.empty((k // 512, 16))
    for p in range(k // 512):
        a[p, :8] = np.random.permutation(np.resize(levels, 8))
        for g in range(8):
            far = levels[np.abs(levels - a[p, g]) >= 10]
            a[p, g + 8] = far[np.random.randint(len(far))]
    return np.exp2(a.ravel()).repeat(32)


def f64(x):
    return np.asarray(x).astype(np.float64)


def planes(y):
    n, m = y.shape
    v = y.astype(np.float32).astype(ml_dtypes.bfloat16).astype(np.float64).reshape(n // 32, 32, m)
    top = np.abs(v).max(1)
    byte = np.clip(np.where(top > 0, np.frexp(top)[1] - 1 + 127 - 7, 1), 1, 254)
    codes = (v * np.exp2(127.0 - byte)[:, None, :]).reshape(n, m).astype(np.float32).astype(ml_dtypes.float8_e4m3fn).view(np.uint8)
    words = codes.reshape(n // 512, 128, 4, m).transpose(0, 1, 3, 2)
    return np.ascontiguousarray(words), np.ascontiguousarray(byte.astype(np.uint8).reshape(n // 512, 16, m))


def split(x):
    m, e = np.frexp(f64(x))
    hi = np.ldexp(np.trunc(16.0 * m) / 16.0, e)
    return hi, f64(x) - hi


K, M, T = 1536, 512, 512


def setup_inputs():
    n = np.random.standard_normal
    s = mx_kscale(K)[:, None]
    return {
        "w": (n((K, M)) / np.sqrt(K) / s).astype(np.float32),
        "x": (n((K, T)) * s).astype(np.float32),
    }


def reference(w, x):
    w_hi, w_lo = split(w)
    w_hi_, w_lo_ = mxq(w_hi, 0, "e4m3"), mxq(w_lo, 0, "e4m3")
    x_hi, x_lo = split(x)
    x_hi_, x_lo_ = mxq(x_hi, 0, "e4m3"), mxq(x_lo, 0, "e4m3")
    y = x_hi_.T @ w_hi_ + x_lo_.T @ w_hi_ + x_hi_.T @ w_lo_
    out_0 = y
    return (out_0,) + planes(out_0)

@@ -1,0 +1,164 @@
+from contextlib import ExitStack
+
+import concourse.mybir as mybir
+
+K, M, T = 1536, 512, 512
+FLOPS = 3 * 2 * K * M * T
+
+F32 = mybir.dt.float32
+BF16 = mybir.dt.bfloat16
+I32 = mybir.dt.int32
+U32 = mybir.dt.uint32
+U8 = mybir.dt.uint8
+FP8X4 = mybir.dt.float8_e4m3fn_x4
+ALU = mybir.AluOpType
+
+P = 128
+PACK = 4
+K_PASS = P * PACK
+PASSES = K // K_PASS
+HALF = M // 2
+PAIR_MASK = -983056
+
+
+def tile_mix_split3_tm_pl_none_kernel(tc, w, x, out_0, out_1, out_2):
+    nc = tc.nc
+    with ExitStack() as ctx:
+        sb = ctx.enter_context(tc.tile_pool(name="sb", bufs=1))
+        ps = ctx.enter_context(tc.psum_pool(name="ps", bufs=1))
+        ctx.enter_context(tc.manual_schedule())
+
+        def sbuf(name, shape, dtype):
+            return sb.tile(shape, dtype, name=name, align_bytes=64)
+
+        order = [("w", 0, 0, 0, 128), ("w", 0, 0, 128, 128), ("w", 0, 1, 0, 256), ("w", 1, 0, 0, 256),
+                 ("x", 0, 0), ("x", 0, 1), ("w", 2, 0, 0, 256), ("x", 1, 0), ("x", 1, 1),
+                 ("x", 2, 0), ("x", 2, 1), ("w", 1, 1, 0, 256), ("w", 2, 1, 0, 256)]
+
+        codes, scales = {}, {}
+        for side in ("w", "x"):
+            for part in ("hi", "lo"):
+                for g in range(PASSES):
+                    for s in range(2):
+                        codes[side, part, g, s] = sbuf("c_%s_%s_%d_%d" % (side, part, g, s), [P, 256], U32)
+                        scales[side, part, g, s] = sbuf("s_%s_%s_%d_%d" % (side, part, g, s), [P, 256], U8)
+
+        raw_x = {}
+        pieces = []
+        for n, piece in enumerate(order):
+            side, g, s = piece[0], piece[1], piece[2]
+            rows = slice(g * K_PASS, (g + 1) * K_PASS)
+            if side == "w":
+                c0, width = piece[3], piece[4]
+                raw = sbuf("raw_%d" % n, [P, PACK, width], F32)
+                cols = slice(s * HALF + c0, s * HALF + c0 + width)
+                nc.sync.dma_start(out=raw[:], in_=w[rows, cols].rearrange("(p j) c -> p j c", j=PACK))
+                value = raw[:].rearrange("p j (c i) -> p c j i", i=2)
+                upper = raw[:].bitcast(BF16).rearrange("p j (c i h) -> p c j i h", i=2, h=2)[:, :, :, :, 1]
+                deal = lambda t: t[:].rearrange("p (c i j) -> p c j i", i=2, j=PACK)
+            else:
+                c0, width = 0, 256
+                if g not in raw_x:
+                    raw_x[g] = sbuf("raw_x%d" % g, [P, PACK, T], F32)
+                    nc.sync.dma_start(out=raw_x[g][:], in_=x[rows, :].rearrange("(p j) t -> p j t", j=PACK))
+                raw = raw_x[g]
+                value = raw[:].rearrange("p j (q r) -> p q j r", r=4)[:, :, :, 2 * s:2 * s + 2]
+                upper = raw[:].bitcast(BF16).rearrange("p j (q r h) -> p q j r h", r=4, h=2)[:, :, :, 2 * s:2 * s + 2, 1]
+                deal = lambda t: t[:].rearrange("p (r q j) -> p q j r", r=2, j=PACK)
+            top = sbuf("top_%d" % n, [P, width * PACK], BF16)
+            hi = sbuf("hi_%d" % n, [P, width * PACK], BF16)
+            lo = sbuf("lo_%d" % n, [P, width * PACK], BF16)
+            pieces.append(dict(side=side, g=g, s=s, cols=slice(c0, c0 + width), value=value, upper=upper,
+                               deal=deal, top=top, hi=hi, lo=lo))
+
+        for pc in pieces:
+            nc.scalar.copy(out=pc["deal"](pc["top"]), in_=pc["upper"])
+
+        acc = {}
+        for h in range(2):
+            for r in range(PACK):
+                acc[h, r] = ps.tile([P, HALF], F32, name="acc_%d_%d" % (h, r))
+        ready = {}
+        done = set()
+        count = {key: 0 for key in acc}
+        products = [("hi", "hi"), ("lo", "hi"), ("hi", "lo")]
+
+        def multiply_ready():
+            for g in range(PASSES):
+                for xp, wp in products:
+                    for h in range(2):
+                        for r in range(PACK):
+                            key = (g, xp, wp, h, r)
+                            xk, wk = ("x", xp, g, r // 2), ("w", wp, g, h)
+                            if key in done or ready.get(xk, 0) < 256 or ready.get(wk, 0) < 256:
+                                continue
+                            done.add(key)
+                            xc = slice((r % 2) * P, (r % 2 + 1) * P)
+                            nc.tensor.matmul_mx(
+                                out=acc[h, r][:], lhsT=codes[xk][:, xc].bitcast(FP8X4), lhsT_scale=scales[xk][:, xc],
+                                rhs=codes[wk][:].bitcast(FP8X4), rhs_scale=scales[wk][:],
+                                start=count[h, r] == 0, stop=count[h, r] == 3 * PASSES - 1)
+                            count[h, r] += 1
+
+        def mask(n):
+            pc = pieces[n]
+            nc.vector.tensor_scalar(out=pc["hi"][:].bitcast(I32), in0=pc["top"][:].bitcast(I32), scalar1=PAIR_MASK,
+                                    scalar2=None, op0=ALU.bitwise_and)
+
+        def subtract(n):
+            pc = pieces[n]
+            nc.vector.tensor_tensor(out=pc["deal"](pc["lo"]), in0=pc["value"], in1=pc["deal"](pc["hi"]), op=ALU.subtract)
+
+        def quantize(n, part):
+            pc = pieces[n]
+            key = (pc["side"], part, pc["g"], pc["s"])
+            nc.vector.quantize_mx(out=codes[key][:, pc["cols"]].bitcast(FP8X4), scales=scales[key][:, pc["cols"]],
+                                  in_=pc[part][:])
+            ready[key] = ready.get(key, 0) + pc["cols"].stop - pc["cols"].start
+            multiply_ready()
+
+        result = [sbuf("result_%d" % h, [P, PACK, HALF], F32) for h in range(2)]
+        rounded = [sbuf("rounded_%d" % h, [P, HALF * PACK], BF16) for h in range(2)]
+        out_words = [sbuf("out_words_%d" % h, [P, HALF], U32) for h in range(2)]
+        out_scales = sbuf("out_scales", [P, M], U8)
+        out_rows = out_0.rearrange("(p i) n -> p i n", i=PACK)
+        word_rows = out_1[0].rearrange("p n i -> p (n i)").bitcast(I32)
+
+        def interleave(h, copy, c0, c1):
+            copy(out=rounded[h][:, c0 * PACK:c1 * PACK].rearrange("p (c e i) -> p c i e", e=2, i=PACK),
+                 in_=result[h][:, :, c0:c1].rearrange("p i (c e) -> p c i e", e=2))
+
+        def quantize_result(h):
+            cols = slice(h * HALF, (h + 1) * HALF)
+            nc.vector.quantize_mx(out=out_words[h][:].bitcast(FP8X4), scales=out_scales[:, cols], in_=rounded[h][:])
+            nc.sync.dma_start(out=word_rows[:, cols], in_=out_words[h][:].bitcast(I32))
+
+        last = len(pieces) - 1
+        mask(0)
+        for n in range(last + 1):
+            if n < last:
+                mask(n + 1)
+            if n > 0:
+                quantize(n - 1, "lo")
+            if n == last - 1:
+                for r in range(PACK):
+                    nc.scalar.copy(out=result[0][:, r, :], in_=acc[0, r][:])
+                nc.sync.dma_start(out=out_rows[:, :, 0:HALF], in_=result[0][:])
+                interleave(0, nc.scalar.copy, 0, HALF)
+            quantize(n, "hi")
+            subtract(n)
+        quantize_result(0)
+        quantize(last, "lo")
+
+        for r in range(PACK):
+            copy = nc.scalar.copy if r % 2 == 0 else nc.vector.tensor_copy
+            copy(out=result[1][:, r, :], in_=acc[1, r][:])
+            if r % 2 == 1:
+                nc.sync.dma_start(out=out_rows[:, r - 1:r + 1, HALF:M], in_=result[1][:, r - 1:r + 1, :])
+        interleave(1, nc.vector.tensor_copy, 0, 160)
+        interleave(1, nc.scalar.copy, 160, HALF)
+        quantize_result(1)
+        for quad in range(4):
+            queue = nc.sync if quad % 2 == 0 else nc.scalar
+            queue.dma_start(out=out_2[0, 4 * quad:4 * quad + 4, :].bitcast(I32),
+                            in_=out_scales[32 * quad:32 * quad + 4, :].bitcast(I32))

@@ -17,8 +17,17 @@ P = 128
 PACK = 4
 K_PASS = P * PACK
 PASSES = K // K_PASS
-HALF = M // 2
+QUARTER = 128
+QUARTERS = M // QUARTER
 PAIR_MASK = -983056
+
+LOADS = [("w", 0, 0, 128), ("w", 0, 128, 128), ("w", 0, 256, 256), ("w", 1, 0, 512),
+         ("x", 0, 0, 512), ("x", 1, 0, 512), ("x", 2, 0, 512), ("w", 2, 0, 512)]
+PIECES = [("w", 0, 0, 128), ("w", 0, 128, 128), ("w", 0, 256, 128), ("w", 0, 384, 128),
+          ("w", 1, 0, 128), ("w", 1, 128, 256),
+          ("x", 0, 0, 256), ("x", 0, 256, 256), ("x", 1, 0, 256), ("x", 2, 0, 256), ("x", 1, 256, 256), ("x", 2, 256, 256),
+          ("w", 2, 0, 128), ("w", 2, 128, 128), ("w", 2, 256, 128), ("w", 1, 384, 128), ("w", 2, 384, 128)]
+PRODUCTS = [("hi", "hi"), ("lo", "hi"), ("hi", "lo")]
 
 
 def tile_mix_split3_tm_pl_none_kernel(tc, w, x, out_0, out_1, out_2):
@@ -31,134 +40,134 @@ def tile_mix_split3_tm_pl_none_kernel(tc, w, x, out_0, out_1, out_2):
         def sbuf(name, shape, dtype):
             return sb.tile(shape, dtype, name=name, align_bytes=64)
 
-        order = [("w", 0, 0, 0, 128), ("w", 0, 0, 128, 128), ("w", 0, 1, 0, 256), ("w", 1, 0, 0, 256),
-                 ("x", 0, 0), ("x", 0, 1), ("w", 2, 0, 0, 256), ("x", 1, 0), ("x", 1, 1),
-                 ("x", 2, 0), ("x", 2, 1), ("w", 1, 1, 0, 256), ("w", 2, 1, 0, 256)]
+        raws = []
+        for n, (side, g, c0, width) in enumerate(LOADS):
+            raw = sbuf("raw_%d" % n, [P, PACK, width], F32)
+            source = w if side == "w" else x
+            nc.sync.dma_start(out=raw[:], in_=source[g * K_PASS:(g + 1) * K_PASS, c0:c0 + width].rearrange("(p j) c -> p j c", j=PACK))
+            raws.append(raw)
 
-        codes, scales = {}, {}
-        for side in ("w", "x"):
-            for part in ("hi", "lo"):
-                for g in range(PASSES):
-                    for s in range(2):
-                        codes[side, part, g, s] = sbuf("c_%s_%s_%d_%d" % (side, part, g, s), [P, 256], U32)
-                        scales[side, part, g, s] = sbuf("s_%s_%s_%d_%d" % (side, part, g, s), [P, 256], U8)
-
-        raw_x = {}
         pieces = []
-        for n, piece in enumerate(order):
-            side, g, s = piece[0], piece[1], piece[2]
-            rows = slice(g * K_PASS, (g + 1) * K_PASS)
+        for n, (side, g, c0, width) in enumerate(PIECES):
+            m = [i for i, ld in enumerate(LOADS) if ld[0] == side and ld[1] == g and ld[2] <= c0 < ld[2] + ld[3]][0]
+            raw = raws[m]
             if side == "w":
-                c0, width = piece[3], piece[4]
-                raw = sbuf("raw_%d" % n, [P, PACK, width], F32)
-                cols = slice(s * HALF + c0, s * HALF + c0 + width)
-                nc.sync.dma_start(out=raw[:], in_=w[rows, cols].rearrange("(p j) c -> p j c", j=PACK))
-                value = raw[:].rearrange("p j (c i) -> p c j i", i=2)
-                upper = raw[:].bitcast(BF16).rearrange("p j (c i h) -> p c j i h", i=2, h=2)[:, :, :, :, 1]
-                deal = lambda t: t[:].rearrange("p (c i j) -> p c j i", i=2, j=PACK)
+                lo_c = (c0 - LOADS[m][2]) // 2
+                pairs = slice(lo_c, lo_c + width // 2)
+                value = raw[:].rearrange("p j (c i) -> p c j i", i=2)[:, pairs]
+                upper = raw[:].bitcast(BF16).rearrange("p j (c i h) -> p c j i h", i=2, h=2)[:, pairs, :, :, 1]
+                deal = lambda t: t.rearrange("p (c i j) -> p c j i", i=2, j=PACK)
             else:
-                c0, width = 0, 256
-                if g not in raw_x:
-                    raw_x[g] = sbuf("raw_x%d" % g, [P, PACK, T], F32)
-                    nc.sync.dma_start(out=raw_x[g][:], in_=x[rows, :].rearrange("(p j) t -> p j t", j=PACK))
-                raw = raw_x[g]
-                value = raw[:].rearrange("p j (q r) -> p q j r", r=4)[:, :, :, 2 * s:2 * s + 2]
-                upper = raw[:].bitcast(BF16).rearrange("p j (q r h) -> p q j r h", r=4, h=2)[:, :, :, 2 * s:2 * s + 2, 1]
-                deal = lambda t: t[:].rearrange("p (r q j) -> p q j r", r=2, j=PACK)
+                rs = slice(c0 // P, c0 // P + 2)
+                value = raw[:].rearrange("p j (q r) -> p q j r", r=4)[:, :, :, rs]
+                upper = raw[:].bitcast(BF16).rearrange("p j (q r h) -> p q j r h", r=4, h=2)[:, :, :, rs, 1]
+                deal = lambda t: t.rearrange("p (r q j) -> p q j r", r=2, j=PACK)
             top = sbuf("top_%d" % n, [P, width * PACK], BF16)
-            hi = sbuf("hi_%d" % n, [P, width * PACK], BF16)
-            lo = sbuf("lo_%d" % n, [P, width * PACK], BF16)
-            pieces.append(dict(side=side, g=g, s=s, cols=slice(c0, c0 + width), value=value, upper=upper,
-                               deal=deal, top=top, hi=hi, lo=lo))
+            parts = sbuf("parts_%d" % n, [P, 2 * width * PACK], BF16)
+            codes = sbuf("codes_%d" % n, [P, 2 * width], U32)
+            scales = sbuf("scales_%d" % n, [P, 2 * width], U8)
+            pieces.append(dict(side=side, g=g, c0=c0, width=width, value=value, upper=upper, deal=deal, top=top,
+                               parts=parts, hi=parts[:, :width * PACK], lo=parts[:, width * PACK:],
+                               codes=codes, scales=scales))
 
         for pc in pieces:
-            nc.scalar.copy(out=pc["deal"](pc["top"]), in_=pc["upper"])
+            nc.scalar.copy(out=pc["deal"](pc["top"][:]), in_=pc["upper"])
 
-        acc = {}
-        for h in range(2):
-            for r in range(PACK):
-                acc[h, r] = ps.tile([P, HALF], F32, name="acc_%d_%d" % (h, r))
+        last_q = QUARTERS - 1
+        banks = {}
+        for c in range(last_q):
+            banks[c, 0] = ps.tile([P, PACK, QUARTER], F32, name="acc_%d" % c)
+        for half in range(2):
+            banks[last_q, half] = ps.tile([P, 2, QUARTER], F32, name="acc_last_%d" % half)
+        count = {key: 0 for key in banks}
         ready = {}
         done = set()
-        count = {key: 0 for key in acc}
-        products = [("hi", "hi"), ("lo", "hi"), ("hi", "lo")]
 
         def multiply_ready():
             for g in range(PASSES):
-                for xp, wp in products:
-                    for h in range(2):
+                for xp, wp in PRODUCTS:
+                    for c in range(QUARTERS):
                         for r in range(PACK):
-                            key = (g, xp, wp, h, r)
-                            xk, wk = ("x", xp, g, r // 2), ("w", wp, g, h)
-                            if key in done or ready.get(xk, 0) < 256 or ready.get(wk, 0) < 256:
+                            key = (g, xp, wp, c, r)
+                            if key in done or ("x", xp, g, r) not in ready or ("w", wp, g, c) not in ready:
                                 continue
                             done.add(key)
-                            xc = slice((r % 2) * P, (r % 2 + 1) * P)
+                            x_codes, x_scales = ready["x", xp, g, r]
+                            w_codes, w_scales = ready["w", wp, g, c]
+                            bank, slot = ((c, r // 2), r % 2) if c == last_q else ((c, 0), r)
+                            total = 3 * PASSES * banks[bank].shape[1]
                             nc.tensor.matmul_mx(
-                                out=acc[h, r][:], lhsT=codes[xk][:, xc].bitcast(FP8X4), lhsT_scale=scales[xk][:, xc],
-                                rhs=codes[wk][:].bitcast(FP8X4), rhs_scale=scales[wk][:],
-                                start=count[h, r] == 0, stop=count[h, r] == 3 * PASSES - 1)
-                            count[h, r] += 1
+                                out=banks[bank][:, slot, :],
+                                lhsT=x_codes.bitcast(FP8X4), lhsT_scale=x_scales,
+                                rhs=w_codes.bitcast(FP8X4), rhs_scale=w_scales,
+                                start=count[bank] == 0, stop=count[bank] == total - 1)
+                            count[bank] += 1
 
         def mask(n):
             pc = pieces[n]
-            nc.vector.tensor_scalar(out=pc["hi"][:].bitcast(I32), in0=pc["top"][:].bitcast(I32), scalar1=PAIR_MASK,
+            nc.vector.tensor_scalar(out=pc["hi"].bitcast(I32), in0=pc["top"][:].bitcast(I32), scalar1=PAIR_MASK,
                                     scalar2=None, op0=ALU.bitwise_and)
 
         def subtract(n):
             pc = pieces[n]
             nc.vector.tensor_tensor(out=pc["deal"](pc["lo"]), in0=pc["value"], in1=pc["deal"](pc["hi"]), op=ALU.subtract)
 
-        def quantize(n, part):
+        def quantize(n, names):
             pc = pieces[n]
-            key = (pc["side"], part, pc["g"], pc["s"])
-            nc.vector.quantize_mx(out=codes[key][:, pc["cols"]].bitcast(FP8X4), scales=scales[key][:, pc["cols"]],
-                                  in_=pc[part][:])
-            ready[key] = ready.get(key, 0) + pc["cols"].stop - pc["cols"].start
+            width = pc["width"]
+            first = 0 if names[0] == "hi" else width
+            cols = slice(first, first + width * len(names))
+            nc.vector.quantize_mx(out=pc["codes"][:, cols].bitcast(FP8X4), scales=pc["scales"][:, cols],
+                                  in_=pc["parts"][:, cols.start * PACK:cols.stop * PACK])
+            for name in names:
+                for c in range(width // P):
+                    at = (0 if name == "hi" else width) + c * P
+                    ready[pc["side"], name, pc["g"], pc["c0"] // P + c] = (pc["codes"][:, at:at + P], pc["scales"][:, at:at + P])
             multiply_ready()
 
-        result = [sbuf("result_%d" % h, [P, PACK, HALF], F32) for h in range(2)]
-        rounded = [sbuf("rounded_%d" % h, [P, HALF * PACK], BF16) for h in range(2)]
-        out_words = [sbuf("out_words_%d" % h, [P, HALF], U32) for h in range(2)]
+        result = [sbuf("result_%d" % c, [P, PACK, QUARTER], F32) for c in range(QUARTERS)]
+        rounded = [sbuf("rounded_%d" % c, [P, QUARTER * PACK], BF16) for c in range(QUARTERS)]
+        out_words = [sbuf("out_words_%d" % c, [P, QUARTER], U32) for c in range(QUARTERS)]
         out_scales = sbuf("out_scales", [P, M], U8)
         out_rows = out_0.rearrange("(p i) n -> p i n", i=PACK)
         word_rows = out_1[0].rearrange("p n i -> p (n i)").bitcast(I32)
 
-        def interleave(h, copy, c0, c1):
-            copy(out=rounded[h][:, c0 * PACK:c1 * PACK].rearrange("p (c e i) -> p c i e", e=2, i=PACK),
-                 in_=result[h][:, :, c0:c1].rearrange("p i (c e) -> p c i e", e=2))
+        def drain(c):
+            nc.scalar.copy(out=rounded[c][:].rearrange("p (n i) -> p n i", i=PACK), in_=banks[c, 0][:].rearrange("p i n -> p n i"))
+            nc.scalar.copy(out=result[c][:], in_=banks[c, 0][:])
+            nc.sync.dma_start(out=out_rows[:, :, c * QUARTER:(c + 1) * QUARTER], in_=result[c][:])
 
-        def quantize_result(h):
-            cols = slice(h * HALF, (h + 1) * HALF)
-            nc.vector.quantize_mx(out=out_words[h][:].bitcast(FP8X4), scales=out_scales[:, cols], in_=rounded[h][:])
-            nc.sync.dma_start(out=word_rows[:, cols], in_=out_words[h][:].bitcast(I32))
+        def quantize_result(c):
+            cols = slice(c * QUARTER, (c + 1) * QUARTER)
+            nc.vector.quantize_mx(out=out_words[c][:].bitcast(FP8X4), scales=out_scales[:, cols], in_=rounded[c][:])
+            nc.sync.dma_start(out=word_rows[:, cols], in_=out_words[c][:].bitcast(I32))
 
         last = len(pieces) - 1
-        mask(0)
+        first_closing = last - 4
         for n in range(last + 1):
-            if n < last:
-                mask(n + 1)
-            if n > 0:
-                quantize(n - 1, "lo")
-            if n == last - 1:
-                for r in range(PACK):
-                    nc.scalar.copy(out=result[0][:, r, :], in_=acc[0, r][:])
-                nc.sync.dma_start(out=out_rows[:, :, 0:HALF], in_=result[0][:])
-                interleave(0, nc.scalar.copy, 0, HALF)
-            quantize(n, "hi")
+            mask(n)
+            if n > first_closing:
+                quantize(n - 1, ["lo"])
+            elif n > 0:
+                quantize(n - 1, ["hi", "lo"])
+            if first_closing < n <= first_closing + 3:
+                drain(n - 1 - first_closing)
+            if n >= first_closing:
+                quantize(n, ["hi"])
             subtract(n)
-        quantize_result(0)
-        quantize(last, "lo")
+            if n >= last - 2:
+                quantize_result(n - (last - 2))
+        quantize(last, ["lo"])
 
-        for r in range(PACK):
-            copy = nc.scalar.copy if r % 2 == 0 else nc.vector.tensor_copy
-            copy(out=result[1][:, r, :], in_=acc[1, r][:])
-            if r % 2 == 1:
-                nc.sync.dma_start(out=out_rows[:, r - 1:r + 1, HALF:M], in_=result[1][:, r - 1:r + 1, :])
-        interleave(1, nc.vector.tensor_copy, 0, 160)
-        interleave(1, nc.scalar.copy, 160, HALF)
-        quantize_result(1)
+        cols = slice(last_q * QUARTER, M)
+        for half, copy in enumerate((nc.scalar.copy, nc.vector.tensor_copy)):
+            rows = slice(2 * half, 2 * half + 2)
+            copy(out=result[last_q][:, rows, :], in_=banks[last_q, half][:])
+            nc.sync.dma_start(out=out_rows[:, rows, cols], in_=result[last_q][:, rows, :])
+        nc.vector.tensor_copy(out=rounded[last_q][:].rearrange("p (c e i) -> p c i e", e=2, i=PACK),
+                              in_=result[last_q][:].rearrange("p i (c e) -> p c i e", e=2))
+        quantize_result(last_q)
         for quad in range(4):
-            queue = nc.sync if quad % 2 == 0 else nc.scalar
+            queue = nc.sync if quad % 2 == 1 else nc.scalar
             queue.dma_start(out=out_2[0, 4 * quad:4 * quad + 4, :].bitcast(I32),
                             in_=out_scales[32 * quad:32 * quad + 4, :].bitcast(I32))

@@ -21,12 +21,17 @@ QUARTER = 128
 QUARTERS = M // QUARTER
 PAIR_MASK = -983056
 
-LOADS = [("w", 0, 0, 128), ("w", 0, 128, 128), ("w", 0, 256, 256), ("w", 1, 0, 512),
-         ("x", 0, 0, 512), ("x", 1, 0, 512), ("x", 2, 0, 512), ("w", 2, 0, 512)]
-PIECES = [("w", 0, 0, 128), ("w", 0, 128, 128), ("w", 0, 256, 128), ("w", 0, 384, 128),
-          ("w", 1, 0, 128), ("w", 1, 128, 256),
-          ("x", 0, 0, 256), ("x", 0, 256, 256), ("x", 1, 0, 256), ("x", 2, 0, 256), ("x", 1, 256, 256), ("x", 2, 256, 256),
-          ("w", 2, 0, 128), ("w", 2, 128, 128), ("w", 2, 256, 128), ("w", 1, 384, 128), ("w", 2, 384, 128)]
+LOADS = [("w", 0, 0, 128), ("w", 0, 128, 128), ("w", 0, 256, 256), ("w", 1, 0, 256),
+         ("x", 0, 0, 512), ("x", 1, 0, 512), ("w", 2, 0, 512), ("w", 1, 256, 256), ("x", 2, 0, 512)]
+UNITS = {"a": [("w", 0, 0, 128)], "b": [("w", 0, 128, 128)], "c": [("w", 0, 256, 128)], "d": [("w", 0, 384, 128)],
+         "e": [("w", 1, 0, 256)], "x0": [("x", 0, 0, 256), ("x", 0, 256, 256)], "x1": [("x", 1, 0, 256), ("x", 1, 256, 256)],
+         "u": [("w", 2, 0, 128), ("w", 2, 128, 128), ("w", 2, 256, 128), ("w", 1, 256, 128)],
+         "x2a": [("x", 2, 0, 256)], "x2b": [("x", 2, 256, 256)],
+         "g": [("w", 1, 384, 128), ("w", 2, 384, 128)]}
+VECTOR = """M a, S a, M b, Q a, S b, M c, S c, M d, Q b, S d, M e, Q c, S e, M x0 0, Q d, S x0 0,
+M x0 1, Q e, S x0 1, M x1, Q x0, S x1 0, S x1 1, M u, Q x1, S u 3, H u, M x2a, L u 3, S x2a,
+M x2b, Q x2a, H x2b, S u 0, S x2b, L u 0, M g, L x2b, D 0, S u 1, S u 2, L u 1, D 1, L u 2, D 2, H g,
+S g 0, O 0, S g 1, L g 0, O 1, L g 1, O 2"""
 PRODUCTS = [("hi", "hi"), ("lo", "hi"), ("hi", "lo")]
 
 
@@ -43,35 +48,44 @@ def tile_mix_split3_tm_pl_none_kernel(tc, w, x, out_0, out_1, out_2):
         raws = []
         for n, (side, g, c0, width) in enumerate(LOADS):
             raw = sbuf("raw_%d" % n, [P, PACK, width], F32)
-            source = w if side == "w" else x
-            nc.sync.dma_start(out=raw[:], in_=source[g * K_PASS:(g + 1) * K_PASS, c0:c0 + width].rearrange("(p j) c -> p j c", j=PACK))
+            operand = w if side == "w" else x
+            nc.sync.dma_start(out=raw[:], in_=operand[g * K_PASS:(g + 1) * K_PASS, c0:c0 + width].rearrange("(p j) c -> p j c", j=PACK))
             raws.append(raw)
 
-        pieces = []
-        for n, (side, g, c0, width) in enumerate(PIECES):
-            m = [i for i, ld in enumerate(LOADS) if ld[0] == side and ld[1] == g and ld[2] <= c0 < ld[2] + ld[3]][0]
-            raw = raws[m]
-            if side == "w":
-                lo_c = (c0 - LOADS[m][2]) // 2
-                pairs = slice(lo_c, lo_c + width // 2)
-                value = raw[:].rearrange("p j (c i) -> p c j i", i=2)[:, pairs]
-                upper = raw[:].bitcast(BF16).rearrange("p j (c i h) -> p c j i h", i=2, h=2)[:, pairs, :, :, 1]
-                deal = lambda t: t.rearrange("p (c i j) -> p c j i", i=2, j=PACK)
-            else:
-                rs = slice(c0 // P, c0 // P + 2)
-                value = raw[:].rearrange("p j (q r) -> p q j r", r=4)[:, :, :, rs]
-                upper = raw[:].bitcast(BF16).rearrange("p j (q r h) -> p q j r h", r=4, h=2)[:, :, :, rs, 1]
-                deal = lambda t: t.rearrange("p (r q j) -> p q j r", r=2, j=PACK)
-            top = sbuf("top_%d" % n, [P, width * PACK], BF16)
-            parts = sbuf("parts_%d" % n, [P, 2 * width * PACK], BF16)
-            codes = sbuf("codes_%d" % n, [P, 2 * width], U32)
-            scales = sbuf("scales_%d" % n, [P, 2 * width], U8)
-            pieces.append(dict(side=side, g=g, c0=c0, width=width, value=value, upper=upper, deal=deal, top=top,
-                               parts=parts, hi=parts[:, :width * PACK], lo=parts[:, width * PACK:],
-                               codes=codes, scales=scales))
+        units = {}
+        for name, segments in UNITS.items():
+            width = sum(seg[3] for seg in segments)
+            starts = [sum(seg[3] for seg in segments[:i]) for i in range(len(segments))]
+            units[name] = dict(segments=segments, starts=starts, width=width,
+                               top=sbuf("top_" + name, [P, width * PACK], BF16),
+                               parts=sbuf("parts_" + name, [P, 2 * width * PACK], BF16),
+                               codes=sbuf("codes_" + name, [P, 2 * width], U32),
+                               scales=sbuf("scales_" + name, [P, 2 * width], U8))
 
-        for pc in pieces:
-            nc.scalar.copy(out=pc["deal"](pc["top"][:]), in_=pc["upper"])
+        def source(segment, halves):
+            side, g, c0, width = segment
+            m = [i for i, ld in enumerate(LOADS) if ld[0] == side and ld[1] == g and ld[2] <= c0 < ld[2] + ld[3]][0]
+            raw = raws[m][:]
+            at = c0 - LOADS[m][2]
+            if side == "w":
+                pairs = slice(at // 2, (at + width) // 2)
+                if halves:
+                    return raw.bitcast(BF16).rearrange("p j (c i h) -> p c j i h", i=2, h=2)[:, pairs, :, :, 1]
+                return raw.rearrange("p j (c i) -> p c j i", i=2)[:, pairs]
+            rs = slice(at // P, at // P + 2)
+            if halves:
+                return raw.bitcast(BF16).rearrange("p j (q r h) -> p q j r h", r=4, h=2)[:, :, :, rs, 1]
+            return raw.rearrange("p j (q r) -> p q j r", r=4)[:, :, :, rs]
+
+        def dealt(segment, tile, at):
+            part = tile[:, at * PACK:(at + segment[3]) * PACK]
+            if segment[0] == "w":
+                return part.rearrange("p (c i j) -> p c j i", i=2, j=PACK)
+            return part.rearrange("p (r q j) -> p q j r", r=2, j=PACK)
+
+        for un in units.values():
+            for segment, at in zip(un["segments"], un["starts"]):
+                nc.scalar.copy(out=dealt(segment, un["top"], at), in_=source(segment, True))
 
         last_q = QUARTERS - 1
         banks = {}
@@ -103,69 +117,82 @@ def tile_mix_split3_tm_pl_none_kernel(tc, w, x, out_0, out_1, out_2):
                                 start=count[bank] == 0, stop=count[bank] == total - 1)
                             count[bank] += 1
 
-        def mask(n):
-            pc = pieces[n]
-            nc.vector.tensor_scalar(out=pc["hi"].bitcast(I32), in0=pc["top"][:].bitcast(I32), scalar1=PAIR_MASK,
-                                    scalar2=None, op0=ALU.bitwise_and)
+        def mask(un, c0, width):
+            cols = slice(c0 * PACK, (c0 + width) * PACK)
+            nc.vector.tensor_scalar(out=un["parts"][:, cols].bitcast(I32), in0=un["top"][:, cols].bitcast(I32),
+                                    scalar1=PAIR_MASK, scalar2=None, op0=ALU.bitwise_and)
 
-        def subtract(n):
-            pc = pieces[n]
-            nc.vector.tensor_tensor(out=pc["deal"](pc["lo"]), in0=pc["value"], in1=pc["deal"](pc["hi"]), op=ALU.subtract)
+        def subtract(un, i):
+            segment, at = un["segments"][i], un["starts"][i]
+            nc.vector.tensor_tensor(out=dealt(segment, un["parts"], un["width"] + at), in0=source(segment, False),
+                                    in1=dealt(segment, un["parts"], at), op=ALU.subtract)
 
-        def quantize(n, names):
-            pc = pieces[n]
-            width = pc["width"]
-            first = 0 if names[0] == "hi" else width
-            cols = slice(first, first + width * len(names))
-            nc.vector.quantize_mx(out=pc["codes"][:, cols].bitcast(FP8X4), scales=pc["scales"][:, cols],
-                                  in_=pc["parts"][:, cols.start * PACK:cols.stop * PACK])
-            for name in names:
-                for c in range(width // P):
-                    at = (0 if name == "hi" else width) + c * P
-                    ready[pc["side"], name, pc["g"], pc["c0"] // P + c] = (pc["codes"][:, at:at + P], pc["scales"][:, at:at + P])
+        def quantize(un, first, width):
+            cols = slice(first, first + width)
+            nc.vector.quantize_mx(out=un["codes"][:, cols].bitcast(FP8X4), scales=un["scales"][:, cols],
+                                  in_=un["parts"][:, cols.start * PACK:cols.stop * PACK])
+            for (side, g, c0, seg_width), start in zip(un["segments"], un["starts"]):
+                for part, name in enumerate(("hi", "lo")):
+                    for c in range(0, seg_width, P):
+                        at = part * un["width"] + start + c
+                        if first <= at < first + width:
+                            ready[side, name, g, (c0 + c) // P] = (un["codes"][:, at:at + P], un["scales"][:, at:at + P])
             multiply_ready()
 
-        result = [sbuf("result_%d" % c, [P, PACK, QUARTER], F32) for c in range(QUARTERS)]
+        first_half = sbuf("result_01", [P, PACK, 2 * QUARTER], F32)
+        result = [first_half[:, :, :QUARTER], first_half[:, :, QUARTER:]]
+        result += [sbuf("result_%d" % c, [P, PACK, QUARTER], F32)[:] for c in (2, 3)]
         rounded = [sbuf("rounded_%d" % c, [P, QUARTER * PACK], BF16) for c in range(QUARTERS)]
-        out_words = [sbuf("out_words_%d" % c, [P, QUARTER], U32) for c in range(QUARTERS)]
+        out_words = sbuf("out_words", [P, M], U32)
         out_scales = sbuf("out_scales", [P, M], U8)
         out_rows = out_0.rearrange("(p i) n -> p i n", i=PACK)
         word_rows = out_1[0].rearrange("p n i -> p (n i)").bitcast(I32)
 
         def drain(c):
+            cols = slice(c * QUARTER, (c + 1) * QUARTER)
+            nc.scalar.copy(out=result[c], in_=banks[c, 0][:])
+            if c == 1:
+                nc.sync.dma_start(out=out_rows[:, :, :cols.stop], in_=first_half[:])
+            if c == 2:
+                nc.sync.dma_start(out=out_rows[:, :, cols], in_=result[c])
             nc.scalar.copy(out=rounded[c][:].rearrange("p (n i) -> p n i", i=PACK), in_=banks[c, 0][:].rearrange("p i n -> p n i"))
-            nc.scalar.copy(out=result[c][:], in_=banks[c, 0][:])
-            nc.sync.dma_start(out=out_rows[:, :, c * QUARTER:(c + 1) * QUARTER], in_=result[c][:])
 
         def quantize_result(c):
             cols = slice(c * QUARTER, (c + 1) * QUARTER)
-            nc.vector.quantize_mx(out=out_words[c][:].bitcast(FP8X4), scales=out_scales[:, cols], in_=rounded[c][:])
-            nc.sync.dma_start(out=word_rows[:, cols], in_=out_words[c][:].bitcast(I32))
+            nc.vector.quantize_mx(out=out_words[:, cols].bitcast(FP8X4), scales=out_scales[:, cols], in_=rounded[c][:])
+            if c % 2 == 1:
+                cols = slice(cols.start - QUARTER, cols.stop)
+                nc.sync.dma_start(out=word_rows[:, cols], in_=out_words[:, cols].bitcast(I32))
 
-        last = len(pieces) - 1
-        first_closing = last - 4
-        for n in range(last + 1):
-            mask(n)
-            if n > first_closing:
-                quantize(n - 1, ["lo"])
-            elif n > 0:
-                quantize(n - 1, ["hi", "lo"])
-            if first_closing < n <= first_closing + 3:
-                drain(n - 1 - first_closing)
-            if n >= first_closing:
-                quantize(n, ["hi"])
-            subtract(n)
-            if n >= last - 2:
-                quantize_result(n - (last - 2))
-        quantize(last, ["lo"])
+        for step in VECTOR.replace("\n", " ").split(","):
+            words = step.split()
+            op = words[0]
+            if op == "D":
+                drain(int(words[1]))
+            elif op == "O":
+                quantize_result(int(words[1]))
+            else:
+                un = units[words[1]]
+                i = int(words[2]) if len(words) > 2 else 0
+                c0, width = (un["starts"][i], un["segments"][i][3]) if len(words) > 2 else (0, un["width"])
+                if op == "M":
+                    mask(un, c0, width)
+                elif op == "S":
+                    subtract(un, i)
+                elif op == "Q":
+                    quantize(un, 0, 2 * width)
+                elif op == "H":
+                    quantize(un, c0, width)
+                else:
+                    quantize(un, un["width"] + c0, width)
 
         cols = slice(last_q * QUARTER, M)
         for half, copy in enumerate((nc.scalar.copy, nc.vector.tensor_copy)):
             rows = slice(2 * half, 2 * half + 2)
             copy(out=result[last_q][:, rows, :], in_=banks[last_q, half][:])
-            nc.sync.dma_start(out=out_rows[:, rows, cols], in_=result[last_q][:, rows, :])
+        nc.sync.dma_start(out=out_rows[:, :, cols], in_=result[last_q])
         nc.vector.tensor_copy(out=rounded[last_q][:].rearrange("p (c e i) -> p c i e", e=2, i=PACK),
-                              in_=result[last_q][:].rearrange("p i (c e) -> p c i e", e=2))
+                              in_=result[last_q].rearrange("p i (c e) -> p c i e", e=2))
         quantize_result(last_q)
         for quad in range(4):
             queue = nc.sync if quad % 2 == 1 else nc.scalar

@@ -1,6 +1,7 @@
 from contextlib import ExitStack
 
 import concourse.mybir as mybir
+from concourse.masks import make_identity
 
 K, M, T = 1536, 512, 512
 FLOPS = 3 * 2 * K * M * T
@@ -20,18 +21,23 @@ PASSES = K // K_PASS
 QUARTER = 128
 QUARTERS = M // QUARTER
 PAIR_MASK = -983056
+HI_MASK = -1048576
+SIGN_BIT = -2147483648
 
 LOADS = [("w", 0, 0, 128), ("w", 0, 128, 128), ("w", 0, 256, 256), ("w", 1, 0, 256),
          ("x", 0, 0, 512), ("x", 1, 0, 512), ("w", 2, 0, 512), ("w", 1, 256, 256), ("x", 2, 0, 512)]
 UNITS = {"a": [("w", 0, 0, 128)], "b": [("w", 0, 128, 128)], "c": [("w", 0, 256, 128)], "d": [("w", 0, 384, 128)],
-         "e": [("w", 1, 0, 256)], "x0": [("x", 0, 0, 256), ("x", 0, 256, 256)], "x1": [("x", 1, 0, 256), ("x", 1, 256, 256)],
-         "u": [("w", 2, 0, 128), ("w", 2, 128, 128), ("w", 2, 256, 128), ("w", 1, 256, 128)],
+         "e": [("w", 1, 0, 256)], "x0a": [("x", 0, 0, 256)], "x0b": [("x", 0, 256, 256)],
+         "x1": [("x", 1, 0, 256), ("x", 1, 256, 256)],
+         "u": [("w", 2, 0, 128), ("w", 2, 128, 128), ("w", 2, 256, 128)], "f": [("w", 1, 256, 128)],
          "x2a": [("x", 2, 0, 256)], "x2b": [("x", 2, 256, 256)],
          "g": [("w", 1, 384, 128), ("w", 2, 384, 128)]}
-VECTOR = """M a, S a, M b, Q a, S b, M c, S c, M d, Q b, S d, M e, Q c, S e, M x0 0, Q d, S x0 0,
-M x0 1, Q e, S x0 1, M x1, Q x0, S x1 0, S x1 1, M u, Q x1, S u 3, H u, M x2a, L u 3, S x2a,
-M x2b, Q x2a, H x2b, S u 0, S x2b, L u 0, M g, L x2b, D 0, S u 1, S u 2, L u 1, D 1, L u 2, D 2, H g,
-S g 0, O 0, S g 1, L g 0, O 1, L g 1, O 2"""
+PROGRAM = """T a, T b, T c, T d, T e, T x0a, T x0b,
+M a, S a, M b, Q a, S b, M c, Q b, S c, M d, Q c, S d, M e, Q d, S e,
+M x0a, Q e, H x0a, N 0, A 0, C 0, M x0b, T u 2, T u 0, S x0a, T f, N 1, C 1, L x0a, S x0b, A 1, M f, H x0b, S f, T u 1, M u 0, H x1,
+T x2a, E 0, S u 0, B 0, E 1, A 2, T x2b, M u 1 2, E 2, L x0b, B 1, L u 0, W 0, M x2a, H u 1 2, S x2a, H u 0, A 3, E 3, Q f, B 2, M x2b, B 3,
+T g 1, Q x2a, W 1, S x2b, H x2b, S u 2, L x2b, L x1, T g 0, F 0, R 0, S u 1, M g, L u 1, L u 2, H g, S g 0, F 1, S g 1, L g 0, L g 1, O 0,
+R 2, O 2, R 1, O 1, F 2"""
 PRODUCTS = [("hi", "hi"), ("lo", "hi"), ("hi", "lo")]
 
 
@@ -40,6 +46,8 @@ def tile_mix_split3_tm_pl_none_kernel(tc, w, x, out_0, out_1, out_2):
     with ExitStack() as ctx:
         sb = ctx.enter_context(tc.tile_pool(name="sb", bufs=1))
         ps = ctx.enter_context(tc.psum_pool(name="ps", bufs=1))
+        identity = sb.tile([P, P], F32, name="identity", align_bytes=64)
+        make_identity(nc, identity[:])
         ctx.enter_context(tc.manual_schedule())
 
         def sbuf(name, shape, dtype):
@@ -83,9 +91,53 @@ def tile_mix_split3_tm_pl_none_kernel(tc, w, x, out_0, out_1, out_2):
                 return part.rearrange("p (c i j) -> p c j i", i=2, j=PACK)
             return part.rearrange("p (r q j) -> p q j r", r=2, j=PACK)
 
-        for un in units.values():
-            for segment, at in zip(un["segments"], un["starts"]):
+        def take_top(un, i, first):
+            segment, at = un["segments"][i], un["starts"][i]
+            if first:
+                nc.scalar.activation(out=dealt(segment, un["top"], at), in_=source(segment, True), func=mybir.ActivationFunctionType.Copy)
+            else:
                 nc.scalar.copy(out=dealt(segment, un["top"], at), in_=source(segment, True))
+
+        raw_t = raws[5]
+        parts_t = units["x1"]["parts"]
+        minus_hi = [sbuf("minus_hi_%d" % h, [P, PACK, 256], F32) for h in range(2)]
+        turned = [sbuf("turned_%d" % m, [P, 512], BF16) for m in range(4)]
+        sums = {}
+        back = {}
+
+        def negate_hi(h):
+            nc.vector.tensor_scalar(out=minus_hi[h][:].bitcast(I32), in0=raw_t[:, :, h * 256:(h + 1) * 256].bitcast(I32),
+                                    scalar1=HI_MASK, scalar2=SIGN_BIT, op0=ALU.bitwise_and, op1=ALU.bitwise_xor)
+
+        def cast_hi(h):
+            out = parts_t[:, :T * PACK].rearrange("p (r q j) -> p q j r", r=4, j=PACK)[:, h * 64:(h + 1) * 64]
+            src = minus_hi[h][:].rearrange("p j (q r) -> p q j r", r=4)
+            for r in (0, 2):
+                nc.scalar.activation(out=out[:, :, :, r:r + 2], in_=src[:, :, :, r:r + 2],
+                                     func=mybir.ActivationFunctionType.Copy, scale=-1.0)
+
+        def turn_and_add(m):
+            sums[m] = ps.tile([P, PACK, P], F32, name="sums_%d" % m, tag="sums", bufs=2)
+            for j in range(PACK):
+                nc.tensor.matmul(out=sums[m][:, j, :], lhsT=raw_t[:, j, m * P:(m + 1) * P], rhs=identity[:],
+                                 start=True, stop=False, is_transpose=True)
+                nc.tensor.matmul(out=sums[m][:, j, :], lhsT=minus_hi[m // 2][:, j, (m % 2) * P:(m % 2 + 1) * P],
+                                 rhs=identity[:], start=False, stop=True, is_transpose=True)
+
+        def round_lo(m):
+            nc.scalar.copy(out=turned[m][:].rearrange("t (u p e) -> t u p e", u=2, e=2),
+                           in_=sums[m][:].rearrange("t (u e) p -> t u p e", e=2))
+
+        def turn_back(m):
+            if m // 2 not in back:
+                back[m // 2] = ps.tile([P, 2, 256], F32, name="back_%d" % (m // 2), tag="back", bufs=1)
+            for u in range(2):
+                nc.tensor.transpose(back[m // 2][:, u, (m % 2) * P:(m % 2 + 1) * P],
+                                    turned[m][:].bitcast(F32)[:, u * P:(u + 1) * P], identity[:])
+
+        def place_lo(h):
+            out = parts_t[:, T * PACK:].bitcast(F32).rearrange("p (r q u) -> p r q u", r=4, u=2)[:, :, h * 64:(h + 1) * 64, :]
+            nc.scalar.copy(out=out, in_=back[h][:].rearrange("p u (q r) -> p r q u", r=4))
 
         last_q = QUARTERS - 1
         banks = {}
@@ -148,13 +200,15 @@ def tile_mix_split3_tm_pl_none_kernel(tc, w, x, out_0, out_1, out_2):
         out_rows = out_0.rearrange("(p i) n -> p i n", i=PACK)
         word_rows = out_1[0].rearrange("p n i -> p (n i)").bitcast(I32)
 
-        def drain(c):
+        def copy_result(c):
             cols = slice(c * QUARTER, (c + 1) * QUARTER)
             nc.scalar.copy(out=result[c], in_=banks[c, 0][:])
             if c == 1:
                 nc.sync.dma_start(out=out_rows[:, :, :cols.stop], in_=first_half[:])
             if c == 2:
                 nc.sync.dma_start(out=out_rows[:, :, cols], in_=result[c])
+
+        def round_result(c):
             nc.scalar.copy(out=rounded[c][:].rearrange("p (n i) -> p n i", i=PACK), in_=banks[c, 0][:].rearrange("p i n -> p n i"))
 
         def quantize_result(c):
@@ -164,27 +218,31 @@ def tile_mix_split3_tm_pl_none_kernel(tc, w, x, out_0, out_1, out_2):
                 cols = slice(cols.start - QUARTER, cols.stop)
                 nc.sync.dma_start(out=word_rows[:, cols], in_=out_words[:, cols].bitcast(I32))
 
-        for step in VECTOR.replace("\n", " ").split(","):
+        by_number = {"F": copy_result, "R": round_result, "O": quantize_result, "N": negate_hi, "C": cast_hi,
+                     "A": turn_and_add, "E": round_lo, "B": turn_back, "W": place_lo}
+        for step in PROGRAM.replace("\n", " ").split(","):
             words = step.split()
             op = words[0]
-            if op == "D":
-                drain(int(words[1]))
-            elif op == "O":
-                quantize_result(int(words[1]))
+            if op in by_number:
+                by_number[op](int(words[1]))
+                continue
+            un = units[words[1]]
+            chosen = [int(word) for word in words[2:]] or list(range(len(un["segments"])))
+            c0 = un["starts"][chosen[0]]
+            width = sum(un["segments"][i][3] for i in chosen)
+            if op == "T":
+                for i in chosen:
+                    take_top(un, i, words[1] == "a")
+            elif op == "M":
+                mask(un, c0, width)
+            elif op == "S":
+                subtract(un, chosen[0])
+            elif op == "Q":
+                quantize(un, 0, 2 * width)
+            elif op == "H":
+                quantize(un, c0, width)
             else:
-                un = units[words[1]]
-                i = int(words[2]) if len(words) > 2 else 0
-                c0, width = (un["starts"][i], un["segments"][i][3]) if len(words) > 2 else (0, un["width"])
-                if op == "M":
-                    mask(un, c0, width)
-                elif op == "S":
-                    subtract(un, i)
-                elif op == "Q":
-                    quantize(un, 0, 2 * width)
-                elif op == "H":
-                    quantize(un, c0, width)
-                else:
-                    quantize(un, un["width"] + c0, width)
+                quantize(un, un["width"] + c0, width)
 
         cols = slice(last_q * QUARTER, M)
         for half, copy in enumerate((nc.scalar.copy, nc.vector.tensor_copy)):

from contextlib import ExitStack

import concourse.mybir as mybir
from concourse.masks import make_identity

K, M, T = 1536, 512, 512
FLOPS = 3 * 2 * K * M * T

F32 = mybir.dt.float32
BF16 = mybir.dt.bfloat16
I32 = mybir.dt.int32
U32 = mybir.dt.uint32
U8 = mybir.dt.uint8
FP8X4 = mybir.dt.float8_e4m3fn_x4
ALU = mybir.AluOpType

P = 128
PACK = 4
K_PASS = P * PACK
PASSES = K // K_PASS
QUARTER = 128
QUARTERS = M // QUARTER
PAIR_MASK = -983056
HI_MASK = -1048576
SIGN_BIT = -2147483648

LOADS = [("w", 0, 0, 128), ("w", 0, 128, 128), ("w", 0, 256, 256), ("w", 1, 0, 256),
         ("x", 0, 0, 512), ("x", 1, 0, 512), ("w", 2, 0, 512), ("w", 1, 256, 256), ("x", 2, 0, 512)]
UNITS = {"a": [("w", 0, 0, 128)], "b": [("w", 0, 128, 128)], "c": [("w", 0, 256, 128)], "d": [("w", 0, 384, 128)],
         "e": [("w", 1, 0, 256)], "x0a": [("x", 0, 0, 256)], "x0b": [("x", 0, 256, 256)],
         "x1": [("x", 1, 0, 256), ("x", 1, 256, 256)],
         "u": [("w", 2, 0, 128), ("w", 2, 128, 128), ("w", 2, 256, 128)], "f": [("w", 1, 256, 128)],
         "x2a": [("x", 2, 0, 256)], "x2b": [("x", 2, 256, 256)],
         "g": [("w", 1, 384, 128), ("w", 2, 384, 128)]}
PROGRAM = """T a, T b, T c, T d, T e, T x0a, T x0b,
M a, S a, M b, Q a, S b, M c, Q b, S c, M d, Q c, S d, M e, Q d, S e,
M x0a, Q e, H x0a, N 0, A 0, C 0, M x0b, T u 2, T u 0, S x0a, T f, N 1, C 1, L x0a, S x0b, A 1, M f, H x0b, S f, T u 1, M u 0, H x1,
T x2a, E 0, S u 0, B 0, E 1, A 2, T x2b, M u 1 2, E 2, L x0b, B 1, L u 0, W 0, M x2a, H u 1 2, S x2a, H u 0, A 3, E 3, Q f, B 2, M x2b, B 3,
T g 1, Q x2a, W 1, S x2b, H x2b, S u 2, L x2b, L x1, T g 0, F 0, R 0, S u 1, M g, L u 1, L u 2, H g, S g 0, F 1, S g 1, L g 0, L g 1, O 0,
R 2, O 2, R 1, O 1, F 2"""
PRODUCTS = [("hi", "hi"), ("lo", "hi"), ("hi", "lo")]


def tile_mix_split3_tm_pl_none_kernel(tc, w, x, out_0, out_1, out_2):
    nc = tc.nc
    with ExitStack() as ctx:
        sb = ctx.enter_context(tc.tile_pool(name="sb", bufs=1))
        ps = ctx.enter_context(tc.psum_pool(name="ps", bufs=1))
        identity = sb.tile([P, P], F32, name="identity", align_bytes=64)
        make_identity(nc, identity[:])
        ctx.enter_context(tc.manual_schedule())

        def sbuf(name, shape, dtype):
            return sb.tile(shape, dtype, name=name, align_bytes=64)

        raws = []
        for n, (side, g, c0, width) in enumerate(LOADS):
            raw = sbuf("raw_%d" % n, [P, PACK, width], F32)
            operand = w if side == "w" else x
            nc.sync.dma_start(out=raw[:], in_=operand[g * K_PASS:(g + 1) * K_PASS, c0:c0 + width].rearrange("(p j) c -> p j c", j=PACK))
            raws.append(raw)

        units = {}
        for name, segments in UNITS.items():
            width = sum(seg[3] for seg in segments)
            starts = [sum(seg[3] for seg in segments[:i]) for i in range(len(segments))]
            units[name] = dict(segments=segments, starts=starts, width=width,
                               top=sbuf("top_" + name, [P, width * PACK], BF16),
                               parts=sbuf("parts_" + name, [P, 2 * width * PACK], BF16),
                               codes=sbuf("codes_" + name, [P, 2 * width], U32),
                               scales=sbuf("scales_" + name, [P, 2 * width], U8))

        def source(segment, halves):
            side, g, c0, width = segment
            m = [i for i, ld in enumerate(LOADS) if ld[0] == side and ld[1] == g and ld[2] <= c0 < ld[2] + ld[3]][0]
            raw = raws[m][:]
            at = c0 - LOADS[m][2]
            if side == "w":
                pairs = slice(at // 2, (at + width) // 2)
                if halves:
                    return raw.bitcast(BF16).rearrange("p j (c i h) -> p c j i h", i=2, h=2)[:, pairs, :, :, 1]
                return raw.rearrange("p j (c i) -> p c j i", i=2)[:, pairs]
            rs = slice(at // P, at // P + 2)
            if halves:
                return raw.bitcast(BF16).rearrange("p j (q r h) -> p q j r h", r=4, h=2)[:, :, :, rs, 1]
            return raw.rearrange("p j (q r) -> p q j r", r=4)[:, :, :, rs]

        def dealt(segment, tile, at):
            part = tile[:, at * PACK:(at + segment[3]) * PACK]
            if segment[0] == "w":
                return part.rearrange("p (c i j) -> p c j i", i=2, j=PACK)
            return part.rearrange("p (r q j) -> p q j r", r=2, j=PACK)

        def take_top(un, i, first):
            segment, at = un["segments"][i], un["starts"][i]
            if first:
                nc.scalar.activation(out=dealt(segment, un["top"], at), in_=source(segment, True), func=mybir.ActivationFunctionType.Copy)
            else:
                nc.scalar.copy(out=dealt(segment, un["top"], at), in_=source(segment, True))

        raw_t = raws[5]
        parts_t = units["x1"]["parts"]
        minus_hi = [sbuf("minus_hi_%d" % h, [P, PACK, 256], F32) for h in range(2)]
        turned = [sbuf("turned_%d" % m, [P, 512], BF16) for m in range(4)]
        sums = {}
        back = {}

        def negate_hi(h):
            nc.vector.tensor_scalar(out=minus_hi[h][:].bitcast(I32), in0=raw_t[:, :, h * 256:(h + 1) * 256].bitcast(I32),
                                    scalar1=HI_MASK, scalar2=SIGN_BIT, op0=ALU.bitwise_and, op1=ALU.bitwise_xor)

        def cast_hi(h):
            out = parts_t[:, :T * PACK].rearrange("p (r q j) -> p q j r", r=4, j=PACK)[:, h * 64:(h + 1) * 64]
            src = minus_hi[h][:].rearrange("p j (q r) -> p q j r", r=4)
            for r in (0, 2):
                nc.scalar.activation(out=out[:, :, :, r:r + 2], in_=src[:, :, :, r:r + 2],
                                     func=mybir.ActivationFunctionType.Copy, scale=-1.0)

        def turn_and_add(m):
            sums[m] = ps.tile([P, PACK, P], F32, name="sums_%d" % m, tag="sums", bufs=2)
            for j in range(PACK):
                nc.tensor.matmul(out=sums[m][:, j, :], lhsT=raw_t[:, j, m * P:(m + 1) * P], rhs=identity[:],
                                 start=True, stop=False, is_transpose=True)
                nc.tensor.matmul(out=sums[m][:, j, :], lhsT=minus_hi[m // 2][:, j, (m % 2) * P:(m % 2 + 1) * P],
                                 rhs=identity[:], start=False, stop=True, is_transpose=True)

        def round_lo(m):
            nc.scalar.copy(out=turned[m][:].rearrange("t (u p e) -> t u p e", u=2, e=2),
                           in_=sums[m][:].rearrange("t (u e) p -> t u p e", e=2))

        def turn_back(m):
            if m // 2 not in back:
                back[m // 2] = ps.tile([P, 2, 256], F32, name="back_%d" % (m // 2), tag="back", bufs=1)
            for u in range(2):
                nc.tensor.transpose(back[m // 2][:, u, (m % 2) * P:(m % 2 + 1) * P],
                                    turned[m][:].bitcast(F32)[:, u * P:(u + 1) * P], identity[:])

        def place_lo(h):
            out = parts_t[:, T * PACK:].bitcast(F32).rearrange("p (r q u) -> p r q u", r=4, u=2)[:, :, h * 64:(h + 1) * 64, :]
            nc.scalar.copy(out=out, in_=back[h][:].rearrange("p u (q r) -> p r q u", r=4))

        last_q = QUARTERS - 1
        banks = {}
        for c in range(last_q):
            banks[c, 0] = ps.tile([P, PACK, QUARTER], F32, name="acc_%d" % c)
        for half in range(2):
            banks[last_q, half] = ps.tile([P, 2, QUARTER], F32, name="acc_last_%d" % half)
        count = {key: 0 for key in banks}
        ready = {}
        done = set()

        def multiply_ready():
            for g in range(PASSES):
                for xp, wp in PRODUCTS:
                    for c in range(QUARTERS):
                        for r in range(PACK):
                            key = (g, xp, wp, c, r)
                            if key in done or ("x", xp, g, r) not in ready or ("w", wp, g, c) not in ready:
                                continue
                            done.add(key)
                            x_codes, x_scales = ready["x", xp, g, r]
                            w_codes, w_scales = ready["w", wp, g, c]
                            bank, slot = ((c, r // 2), r % 2) if c == last_q else ((c, 0), r)
                            total = 3 * PASSES * banks[bank].shape[1]
                            nc.tensor.matmul_mx(
                                out=banks[bank][:, slot, :],
                                lhsT=x_codes.bitcast(FP8X4), lhsT_scale=x_scales,
                                rhs=w_codes.bitcast(FP8X4), rhs_scale=w_scales,
                                start=count[bank] == 0, stop=count[bank] == total - 1)
                            count[bank] += 1

        def mask(un, c0, width):
            cols = slice(c0 * PACK, (c0 + width) * PACK)
            nc.vector.tensor_scalar(out=un["parts"][:, cols].bitcast(I32), in0=un["top"][:, cols].bitcast(I32),
                                    scalar1=PAIR_MASK, scalar2=None, op0=ALU.bitwise_and)

        def subtract(un, i):
            segment, at = un["segments"][i], un["starts"][i]
            nc.vector.tensor_tensor(out=dealt(segment, un["parts"], un["width"] + at), in0=source(segment, False),
                                    in1=dealt(segment, un["parts"], at), op=ALU.subtract)

        def quantize(un, first, width):
            cols = slice(first, first + width)
            nc.vector.quantize_mx(out=un["codes"][:, cols].bitcast(FP8X4), scales=un["scales"][:, cols],
                                  in_=un["parts"][:, cols.start * PACK:cols.stop * PACK])
            for (side, g, c0, seg_width), start in zip(un["segments"], un["starts"]):
                for part, name in enumerate(("hi", "lo")):
                    for c in range(0, seg_width, P):
                        at = part * un["width"] + start + c
                        if first <= at < first + width:
                            ready[side, name, g, (c0 + c) // P] = (un["codes"][:, at:at + P], un["scales"][:, at:at + P])
            multiply_ready()

        first_half = sbuf("result_01", [P, PACK, 2 * QUARTER], F32)
        result = [first_half[:, :, :QUARTER], first_half[:, :, QUARTER:]]
        result += [sbuf("result_%d" % c, [P, PACK, QUARTER], F32)[:] for c in (2, 3)]
        rounded = [sbuf("rounded_%d" % c, [P, QUARTER * PACK], BF16) for c in range(QUARTERS)]
        out_words = sbuf("out_words", [P, M], U32)
        out_scales = sbuf("out_scales", [P, M], U8)
        out_rows = out_0.rearrange("(p i) n -> p i n", i=PACK)
        word_rows = out_1[0].rearrange("p n i -> p (n i)").bitcast(I32)

        def copy_result(c):
            cols = slice(c * QUARTER, (c + 1) * QUARTER)
            nc.scalar.copy(out=result[c], in_=banks[c, 0][:])
            if c == 1:
                nc.sync.dma_start(out=out_rows[:, :, :cols.stop], in_=first_half[:])
            if c == 2:
                nc.sync.dma_start(out=out_rows[:, :, cols], in_=result[c])

        def round_result(c):
            nc.scalar.copy(out=rounded[c][:].rearrange("p (n i) -> p n i", i=PACK), in_=banks[c, 0][:].rearrange("p i n -> p n i"))

        def quantize_result(c):
            cols = slice(c * QUARTER, (c + 1) * QUARTER)
            nc.vector.quantize_mx(out=out_words[:, cols].bitcast(FP8X4), scales=out_scales[:, cols], in_=rounded[c][:])
            if c % 2 == 1:
                cols = slice(cols.start - QUARTER, cols.stop)
                nc.sync.dma_start(out=word_rows[:, cols], in_=out_words[:, cols].bitcast(I32))

        by_number = {"F": copy_result, "R": round_result, "O": quantize_result, "N": negate_hi, "C": cast_hi,
                     "A": turn_and_add, "E": round_lo, "B": turn_back, "W": place_lo}
        for step in PROGRAM.replace("\n", " ").split(","):
            words = step.split()
            op = words[0]
            if op in by_number:
                by_number[op](int(words[1]))
                continue
            un = units[words[1]]
            chosen = [int(word) for word in words[2:]] or list(range(len(un["segments"])))
            c0 = un["starts"][chosen[0]]
            width = sum(un["segments"][i][3] for i in chosen)
            if op == "T":
                for i in chosen:
                    take_top(un, i, words[1] == "a")
            elif op == "M":
                mask(un, c0, width)
            elif op == "S":
                subtract(un, chosen[0])
            elif op == "Q":
                quantize(un, 0, 2 * width)
            elif op == "H":
                quantize(un, c0, width)
            else:
                quantize(un, un["width"] + c0, width)

        cols = slice(last_q * QUARTER, M)
        for half, copy in enumerate((nc.scalar.copy, nc.vector.tensor_copy)):
            rows = slice(2 * half, 2 * half + 2)
            copy(out=result[last_q][:, rows, :], in_=banks[last_q, half][:])
        nc.sync.dma_start(out=out_rows[:, :, cols], in_=result[last_q])
        nc.vector.tensor_copy(out=rounded[last_q][:].rearrange("p (c e i) -> p c i e", e=2, i=PACK),
                              in_=result[last_q].rearrange("p i (c e) -> p c i e", e=2))
        quantize_result(last_q)
        for quad in range(4):
            queue = nc.sync if quad % 2 == 1 else nc.scalar
            queue.dma_start(out=out_2[0, 4 * quad:4 * quad + 4, :].bitcast(I32),
                            in_=out_scales[32 * quad:32 * quad + 4, :].bitcast(I32))
